import numpy as np
import ml_dtypes


def mxq(x, axis, fmt="e4m3"):
    dtype, down = {"e4m3": (ml_dtypes.float8_e4m3fn, 7), "e5m2": (ml_dtypes.float8_e5m2, 14)}[fmt]
    v = np.moveaxis(np.asarray(x, np.float32).astype(ml_dtypes.bfloat16).astype(np.float64), axis, -1)
    blocks = v.reshape(v.shape[:-1] + (-1, 32))
    amax = np.abs(blocks).max(-1, keepdims=True)
    byte = np.maximum(np.where(amax > 0, np.frexp(amax)[1] - 1 + 127, 0) - down, 1)
    scale = np.exp2(byte - 127.0)
    codes = (blocks / scale).astype(np.float32).astype(dtype).astype(np.float64)
    return np.moveaxis((codes * scale).reshape(v.shape), -1, axis)


WIDE = False


def mx_kscale(k):
    if not WIDE:
        return np.ones(k)
    levels = np.array([10, -10, 5, -5, 0])
    if k % 512:
        return np.exp2(np.random.permutation(np.resize(levels, k // 32))).repeat(32)
    a = np.empty((k // 512, 16))
    for p in range(k // 512):
        a[p, :8] = np.random.permutation(np.resize(levels, 8))
        for g in range(8):
            far = levels[np.abs(levels - a[p, g]) >= 10]
            a[p, g + 8] = far[np.random.randint(len(far))]
    return np.exp2(a.ravel()).repeat(32)


def f64(x):
    return np.asarray(x).astype(np.float64)


def striped(idx):
    return np.tile(idx.reshape(-1, 16).T, (8, 1)).astype(np.uint16)


def unstriped(offs):
    return offs[:16].T.reshape(-1).astype(np.int64)


K, T, S, N = 1024, 2048, 512, 128


def setup_inputs():
    n = np.random.standard_normal
    s = mx_kscale(K)[:, None]
    w1, w2 = n((2, K, N)) / np.sqrt(2 * K) / s[None]
    return {
        "xT": (n((K, S)) * s).astype(np.float32),
        "sT": (n((K, T)) * s).astype(np.float32),
        "w1": w1.astype(np.float32),
        "w2": w2.astype(np.float32),
        "offs": striped(np.random.permutation(T)[:S]),
    }


def reference(xT, sT, w1, w2, offs):
    y = mxq(f64(w1), 0, "e4m3").T @ mxq(f64(xT), 0, "e4m3") + mxq(f64(w2), 0, "e4m3").T @ mxq(f64(sT)[:, unstriped(offs)], 0, "e4m3")
    return y

@@ -1,0 +1,120 @@
+from contextlib import ExitStack
+
+import concourse.mybir as mybir
+
+K, T, S, N = 1024, 2048, 512, 128
+FLOPS = 2 * 2 * K * N * S
+
+F32 = mybir.dt.float32
+BF16 = mybir.dt.bfloat16
+U32 = mybir.dt.uint32
+U16 = mybir.dt.uint16
+U8 = mybir.dt.uint8
+FP8X4 = mybir.dt.float8_e4m3fn_x4
+
+P = 128
+PACK = 4
+K_PASS = P * PACK
+PASSES = K // K_PASS
+GROUPS = [(0, 256), (256, 384), (384, 512)]
+
+
+def interleave(copy, grouped, raw):
+    copy(
+        grouped.rearrange("p (c i) t -> p c t i", i=4),
+        raw.rearrange("p t (c i) -> p c t i", i=4),
+    )
+
+
+def tile_picked_recall_none_e_kernel(tc, xT, sT, w1, w2, offs, out):
+    nc = tc.nc
+    with ExitStack() as ctx:
+        pool = ctx.enter_context(tc.tile_pool(name="held", bufs=1))
+        psum = ctx.enter_context(tc.psum_pool(name="psum", bufs=1))
+
+        def quantize(name, grouped, width):
+            codes = pool.tile([P, width], U32, name=name + "_codes", align_bytes=64)
+            scales = pool.tile([P, width], U8, name=name + "_scales", align_bytes=64)
+            nc.vector.quantize_mx(out=codes[:].bitcast(FP8X4), scales=scales[:], in_=grouped)
+            return codes, scales
+
+        offsets = pool.tile([P, S // 16], U16, name="offsets")
+        s_rows = sT.rearrange("(a p t) c -> a t p c", a=PASSES, t=PACK)
+        x_rows = xT.rearrange("(a p t) c -> a p t c", a=PASSES, t=PACK)
+
+        planes = {}
+
+        def load_plane(a, t):
+            plane = pool.tile([P, T], F32, name=f"plane{a}{t}")
+            nc.sync.dma_start(plane[:], s_rows[a, t])
+            planes[(a, t)] = plane
+
+        load_plane(0, 0)
+        nc.sync.dma_start(offsets[:], offs)
+        for t in range(1, PACK):
+            load_plane(0, t)
+        w_raw = []
+        for name, w in (("w2_raw", w2), ("w1_raw", w1)):
+            raw = pool.tile([P, PASSES, PACK, N], F32, name=name)
+            nc.sync.dma_start(
+                raw[:].rearrange("p a t m -> p a (t m)"),
+                w.rearrange("(a p t) m -> p a (t m)", a=PASSES, t=PACK),
+            )
+            w_raw.append(raw)
+        for t in range(PACK):
+            load_plane(1, t)
+        x0_raw = pool.tile([P, PACK, S], F32, name="x0_raw")
+        nc.sync.dma_start(x0_raw[:], x_rows[0])
+        x1_raw = []
+        for g, (lo, hi) in enumerate(GROUPS):
+            raw = pool.tile([P, PACK, hi - lo], F32, name=f"x1_raw{g}")
+            nc.sync.dma_start(raw[:], x_rows[1][:, :, lo:hi])
+            x1_raw.append(raw)
+
+        def gather_pass(a):
+            grouped = pool.tile([P, S, PACK], BF16, name=f"s{a}_grouped", align_bytes=64)
+            for t in range(PACK):
+                nc.vector.tensor_copy(grouped[:, :, t], planes[(a, t)][:].indirect(offsets[:]))
+            return quantize(f"s{a}", grouped[:].rearrange("p c t -> p (c t)"), S)
+
+        s0_q = gather_pass(0)
+        w_q = []
+        for name, raw in zip(("w2", "w1"), w_raw):
+            grouped = pool.tile([P, PASSES, N, PACK], BF16, name=name + "_grouped", align_bytes=64)
+            for a in range(PASSES):
+                interleave(nc.scalar.copy, grouped[:, a], raw[:, a])
+            w_q.append(quantize(name, grouped[:].rearrange("p a m t -> p (a m t)"), PASSES * N))
+        w2_q, w1_q = w_q
+        s1_q = gather_pass(1)
+        x0_grouped = pool.tile([P, S, PACK], BF16, name="x0_grouped", align_bytes=64)
+        interleave(nc.scalar.copy, x0_grouped[:, :192], x0_raw[:, :, :192])
+        interleave(nc.vector.tensor_copy, x0_grouped[:, 192:], x0_raw[:, :, 192:])
+        x0_q = quantize("x0", x0_grouped[:].rearrange("p c t -> p (c t)"), S)
+
+        def mx_pass(acc, weights, a, moving, lo, hi, start, stop):
+            nc.tensor.matmul_mx(
+                out=acc[:],
+                lhsT=weights[0][:, a * N : (a + 1) * N].bitcast(FP8X4),
+                lhsT_scale=weights[1][:, a * N : (a + 1) * N],
+                rhs=moving[0][:, lo:hi].bitcast(FP8X4),
+                rhs_scale=moving[1][:, lo:hi],
+                start=start,
+                stop=stop,
+            )
+
+        accs = [psum.tile([N, hi - lo], F32, name=f"acc{g}") for g, (lo, hi) in enumerate(GROUPS)]
+        for step, (weights, a, moving) in enumerate(((w2_q, 0, s0_q), (w2_q, 1, s1_q), (w1_q, 0, x0_q))):
+            for acc, (lo, hi) in zip(accs, GROUPS):
+                mx_pass(acc, weights, a, moving, lo, hi, step == 0, False)
+
+        casts = (nc.scalar.copy, nc.vector.tensor_copy, nc.vector.tensor_copy)
+        drains = (nc.scalar.copy, nc.scalar.copy, nc.vector.tensor_copy)
+        for g, (lo, hi) in enumerate(GROUPS):
+            width = hi - lo
+            grouped = pool.tile([P, width, PACK], BF16, name=f"x1_grouped{g}", align_bytes=64)
+            interleave(casts[g], grouped[:], x1_raw[g][:])
+            x1_q = quantize(f"x1_{g}", grouped[:].rearrange("p c t -> p (c t)"), width)
+            mx_pass(accs[g], w1_q, 1, x1_q, 0, width, False, True)
+            result = pool.tile([N, width], F32, name=f"result{g}")
+            drains[g](result[:], accs[g][:])
+            nc.sync.dma_start(out[:, lo:hi], result[:])

@@ -16,7 +16,7 @@ P = 128
 PACK = 4
 K_PASS = P * PACK
 PASSES = K // K_PASS
-GROUPS = [(0, 256), (256, 384), (384, 512)]
+GROUPS = [(0, 256, 128), (256, 384, 128), (384, 512, 48)]
 
 
 def interleave(copy, grouped, raw):
@@ -39,57 +39,65 @@ def tile_picked_recall_none_e_kernel(tc, xT, sT, w1, w2, offs, out):
             return codes, scales
 
         offsets = pool.tile([P, S // 16], U16, name="offsets")
-        s_rows = sT.rearrange("(a p t) c -> a t p c", a=PASSES, t=PACK)
+        s_rows = sT.rearrange("(a p t) c -> a p t c", a=PASSES, t=PACK)
         x_rows = xT.rearrange("(a p t) c -> a p t c", a=PASSES, t=PACK)
 
         planes = {}
 
-        def load_plane(a, t):
-            plane = pool.tile([P, T], F32, name=f"plane{a}{t}")
-            nc.sync.dma_start(plane[:], s_rows[a, t])
-            planes[(a, t)] = plane
+        def load_planes(a, first, count):
+            tile = pool.tile([P, count, T], F32, name=f"planes{a}{first}")
+            nc.sync.dma_start(tile[:], s_rows[a][:, first : first + count, :])
+            for t in range(count):
+                planes[(a, first + t)] = tile[:, t, :]
 
-        load_plane(0, 0)
-        nc.sync.dma_start(offsets[:], offs)
-        for t in range(1, PACK):
-            load_plane(0, t)
-        w_raw = []
-        for name, w in (("w2_raw", w2), ("w1_raw", w1)):
+        def load_weights(name, w):
             raw = pool.tile([P, PASSES, PACK, N], F32, name=name)
             nc.sync.dma_start(
                 raw[:].rearrange("p a t m -> p a (t m)"),
                 w.rearrange("(a p t) m -> p a (t m)", a=PASSES, t=PACK),
             )
-            w_raw.append(raw)
-        for t in range(PACK):
-            load_plane(1, t)
+            return raw
+
+        load_planes(0, 0, 2)
+        nc.sync.dma_start(offsets[:], offs)
+        load_planes(0, 2, 2)
+        w2_raw = load_weights("w2_raw", w2)
+        load_planes(1, 0, 2)
         x0_raw = pool.tile([P, PACK, S], F32, name="x0_raw")
         nc.sync.dma_start(x0_raw[:], x_rows[0])
+        load_planes(1, 2, 1)
+        load_planes(1, 3, 1)
+        w1_raw = load_weights("w1_raw", w1)
         x1_raw = []
-        for g, (lo, hi) in enumerate(GROUPS):
+        for g, (lo, hi, share) in enumerate(GROUPS):
             raw = pool.tile([P, PACK, hi - lo], F32, name=f"x1_raw{g}")
             nc.sync.dma_start(raw[:], x_rows[1][:, :, lo:hi])
             x1_raw.append(raw)
 
-        def gather_pass(a):
-            grouped = pool.tile([P, S, PACK], BF16, name=f"s{a}_grouped", align_bytes=64)
-            for t in range(PACK):
-                nc.vector.tensor_copy(grouped[:, :, t], planes[(a, t)][:].indirect(offsets[:]))
-            return quantize(f"s{a}", grouped[:].rearrange("p c t -> p (c t)"), S)
-
-        s0_q = gather_pass(0)
-        w_q = []
-        for name, raw in zip(("w2", "w1"), w_raw):
+        def weights_quantized(name, raw):
             grouped = pool.tile([P, PASSES, N, PACK], BF16, name=name + "_grouped", align_bytes=64)
             for a in range(PASSES):
                 interleave(nc.scalar.copy, grouped[:, a], raw[:, a])
-            w_q.append(quantize(name, grouped[:].rearrange("p a m t -> p (a m t)"), PASSES * N))
-        w2_q, w1_q = w_q
-        s1_q = gather_pass(1)
+            return quantize(name, grouped[:].rearrange("p a m t -> p (a m t)"), PASSES * N)
+
+        s0_picked = pool.tile([P, PACK, S], F32, name="s0_picked")
+        for t in range(PACK):
+            nc.vector.tensor_copy(s0_picked[:, t, :], planes[(0, t)].indirect(offsets[:]))
+        w2_q = weights_quantized("w2", w2_raw)
+        s0_grouped = pool.tile([P, S, PACK], BF16, name="s0_grouped", align_bytes=64)
+        interleave(nc.scalar.copy, s0_grouped[:], s0_picked[:])
+        s0_q = quantize("s0", s0_grouped[:].rearrange("p c t -> p (c t)"), S)
+
+        s1_grouped = pool.tile([P, S, PACK], BF16, name="s1_grouped", align_bytes=64)
+        for t in range(2):
+            nc.vector.tensor_copy(s1_grouped[:, :, t], planes[(1, t)].indirect(offsets[:]))
         x0_grouped = pool.tile([P, S, PACK], BF16, name="x0_grouped", align_bytes=64)
-        interleave(nc.scalar.copy, x0_grouped[:, :192], x0_raw[:, :, :192])
-        interleave(nc.vector.tensor_copy, x0_grouped[:, 192:], x0_raw[:, :, 192:])
+        interleave(nc.scalar.copy, x0_grouped[:], x0_raw[:])
         x0_q = quantize("x0", x0_grouped[:].rearrange("p c t -> p (c t)"), S)
+        for t in range(2, PACK):
+            nc.vector.tensor_copy(s1_grouped[:, :, t], planes[(1, t)].indirect(offsets[:]))
+        s1_q = quantize("s1", s1_grouped[:].rearrange("p c t -> p (c t)"), S)
+        w1_q = weights_quantized("w1", w1_raw)
 
         def mx_pass(acc, weights, a, moving, lo, hi, start, stop):
             nc.tensor.matmul_mx(
@@ -102,17 +110,18 @@ def tile_picked_recall_none_e_kernel(tc, xT, sT, w1, w2, offs, out):
                 stop=stop,
             )
 
-        accs = [psum.tile([N, hi - lo], F32, name=f"acc{g}") for g, (lo, hi) in enumerate(GROUPS)]
+        accs = [psum.tile([N, hi - lo], F32, name=f"acc{g}") for g, (lo, hi, share) in enumerate(GROUPS)]
         for step, (weights, a, moving) in enumerate(((w2_q, 0, s0_q), (w2_q, 1, s1_q), (w1_q, 0, x0_q))):
-            for acc, (lo, hi) in zip(accs, GROUPS):
+            for acc, (lo, hi, share) in zip(accs, GROUPS):
                 mx_pass(acc, weights, a, moving, lo, hi, step == 0, False)
 
-        casts = (nc.scalar.copy, nc.vector.tensor_copy, nc.vector.tensor_copy)
-        drains = (nc.scalar.copy, nc.scalar.copy, nc.vector.tensor_copy)
-        for g, (lo, hi) in enumerate(GROUPS):
+        drains = (nc.scalar.copy, nc.vector.tensor_copy, nc.scalar.copy)
+        for g, (lo, hi, share) in enumerate(GROUPS):
             width = hi - lo
             grouped = pool.tile([P, width, PACK], BF16, name=f"x1_grouped{g}", align_bytes=64)
-            interleave(casts[g], grouped[:], x1_raw[g][:])
+            interleave(nc.scalar.copy, grouped[:, :share], x1_raw[g][:, :, :share])
+            if share < width:
+                interleave(nc.vector.tensor_copy, grouped[:, share:], x1_raw[g][:, :, share:])
             x1_q = quantize(f"x1_{g}", grouped[:].rearrange("p c t -> p (c t)"), width)
             mx_pass(accs[g], w1_q, 1, x1_q, 0, width, False, True)
             result = pool.tile([N, width], F32, name=f"result{g}")

from contextlib import ExitStack

import concourse.mybir as mybir

K, T, S, N = 1024, 2048, 512, 128
FLOPS = 2 * 2 * K * N * S

F32 = mybir.dt.float32
BF16 = mybir.dt.bfloat16
U32 = mybir.dt.uint32
U16 = mybir.dt.uint16
U8 = mybir.dt.uint8
FP8X4 = mybir.dt.float8_e4m3fn_x4

P = 128
PACK = 4
K_PASS = P * PACK
PASSES = K // K_PASS
GROUPS = [(0, 256, 128), (256, 384, 128), (384, 512, 48)]


def interleave(copy, grouped, raw):
    copy(
        grouped.rearrange("p (c i) t -> p c t i", i=4),
        raw.rearrange("p t (c i) -> p c t i", i=4),
    )


def tile_picked_recall_none_e_kernel(tc, xT, sT, w1, w2, offs, out):
    nc = tc.nc
    with ExitStack() as ctx:
        pool = ctx.enter_context(tc.tile_pool(name="held", bufs=1))
        psum = ctx.enter_context(tc.psum_pool(name="psum", bufs=1))

        def quantize(name, grouped, width):
            codes = pool.tile([P, width], U32, name=name + "_codes", align_bytes=64)
            scales = pool.tile([P, width], U8, name=name + "_scales", align_bytes=64)
            nc.vector.quantize_mx(out=codes[:].bitcast(FP8X4), scales=scales[:], in_=grouped)
            return codes, scales

        offsets = pool.tile([P, S // 16], U16, name="offsets")
        s_rows = sT.rearrange("(a p t) c -> a p t c", a=PASSES, t=PACK)
        x_rows = xT.rearrange("(a p t) c -> a p t c", a=PASSES, t=PACK)

        planes = {}

        def load_planes(a, first, count):
            tile = pool.tile([P, count, T], F32, name=f"planes{a}{first}")
            nc.sync.dma_start(tile[:], s_rows[a][:, first : first + count, :])
            for t in range(count):
                planes[(a, first + t)] = tile[:, t, :]

        def load_weights(name, w):
            raw = pool.tile([P, PASSES, PACK, N], F32, name=name)
            nc.sync.dma_start(
                raw[:].rearrange("p a t m -> p a (t m)"),
                w.rearrange("(a p t) m -> p a (t m)", a=PASSES, t=PACK),
            )
            return raw

        load_planes(0, 0, 2)
        nc.sync.dma_start(offsets[:], offs)
        load_planes(0, 2, 2)
        w2_raw = load_weights("w2_raw", w2)
        load_planes(1, 0, 2)
        x0_raw = pool.tile([P, PACK, S], F32, name="x0_raw")
        nc.sync.dma_start(x0_raw[:], x_rows[0])
        load_planes(1, 2, 1)
        load_planes(1, 3, 1)
        w1_raw = load_weights("w1_raw", w1)
        x1_raw = []
        for g, (lo, hi, share) in enumerate(GROUPS):
            raw = pool.tile([P, PACK, hi - lo], F32, name=f"x1_raw{g}")
            nc.sync.dma_start(raw[:], x_rows[1][:, :, lo:hi])
            x1_raw.append(raw)

        def weights_quantized(name, raw):
            grouped = pool.tile([P, PASSES, N, PACK], BF16, name=name + "_grouped", align_bytes=64)
            for a in range(PASSES):
                interleave(nc.scalar.copy, grouped[:, a], raw[:, a])
            return quantize(name, grouped[:].rearrange("p a m t -> p (a m t)"), PASSES * N)

        s0_picked = pool.tile([P, PACK, S], F32, name="s0_picked")
        for t in range(PACK):
            nc.vector.tensor_copy(s0_picked[:, t, :], planes[(0, t)].indirect(offsets[:]))
        w2_q = weights_quantized("w2", w2_raw)
        s0_grouped = pool.tile([P, S, PACK], BF16, name="s0_grouped", align_bytes=64)
        interleave(nc.scalar.copy, s0_grouped[:], s0_picked[:])
        s0_q = quantize("s0", s0_grouped[:].rearrange("p c t -> p (c t)"), S)

        s1_grouped = pool.tile([P, S, PACK], BF16, name="s1_grouped", align_bytes=64)
        for t in range(2):
            nc.vector.tensor_copy(s1_grouped[:, :, t], planes[(1, t)].indirect(offsets[:]))
        x0_grouped = pool.tile([P, S, PACK], BF16, name="x0_grouped", align_bytes=64)
        interleave(nc.scalar.copy, x0_grouped[:], x0_raw[:])
        x0_q = quantize("x0", x0_grouped[:].rearrange("p c t -> p (c t)"), S)
        for t in range(2, PACK):
            nc.vector.tensor_copy(s1_grouped[:, :, t], planes[(1, t)].indirect(offsets[:]))
        s1_q = quantize("s1", s1_grouped[:].rearrange("p c t -> p (c t)"), S)
        w1_q = weights_quantized("w1", w1_raw)

        def mx_pass(acc, weights, a, moving, lo, hi, start, stop):
            nc.tensor.matmul_mx(
                out=acc[:],
                lhsT=weights[0][:, a * N : (a + 1) * N].bitcast(FP8X4),
                lhsT_scale=weights[1][:, a * N : (a + 1) * N],
                rhs=moving[0][:, lo:hi].bitcast(FP8X4),
                rhs_scale=moving[1][:, lo:hi],
                start=start,
                stop=stop,
            )

        accs = [psum.tile([N, hi - lo], F32, name=f"acc{g}") for g, (lo, hi, share) in enumerate(GROUPS)]
        for step, (weights, a, moving) in enumerate(((w2_q, 0, s0_q), (w2_q, 1, s1_q), (w1_q, 0, x0_q))):
            for acc, (lo, hi, share) in zip(accs, GROUPS):
                mx_pass(acc, weights, a, moving, lo, hi, step == 0, False)

        drains = (nc.scalar.copy, nc.vector.tensor_copy, nc.scalar.copy)
        for g, (lo, hi, share) in enumerate(GROUPS):
            width = hi - lo
            grouped = pool.tile([P, width, PACK], BF16, name=f"x1_grouped{g}", align_bytes=64)
            interleave(nc.scalar.copy, grouped[:, :share], x1_raw[g][:, :, :share])
            if share < width:
                interleave(nc.vector.tensor_copy, grouped[:, share:], x1_raw[g][:, :, share:])
            x1_q = quantize(f"x1_{g}", grouped[:].rearrange("p c t -> p (c t)"), width)
            mx_pass(accs[g], w1_q, 1, x1_q, 0, width, False, True)
            result = pool.tile([N, width], F32, name=f"result{g}")
            drains[g](result[:], accs[g][:])
            nc.sync.dma_start(out[:, lo:hi], result[:])
